import numpy as np
import ml_dtypes


def mxq(x, axis, fmt="e4m3"):
    dtype, down = {"e4m3": (ml_dtypes.float8_e4m3fn, 7), "e5m2": (ml_dtypes.float8_e5m2, 14)}[fmt]
    v = np.moveaxis(np.asarray(x, np.float32).astype(ml_dtypes.bfloat16).astype(np.float64), axis, -1)
    blocks = v.reshape(v.shape[:-1] + (-1, 32))
    amax = np.abs(blocks).max(-1, keepdims=True)
    byte = np.maximum(np.where(amax > 0, np.frexp(amax)[1] - 1 + 127, 0) - down, 1)
    scale = np.exp2(byte - 127.0)
    codes = (blocks / scale).astype(np.float32).astype(dtype).astype(np.float64)
    return np.moveaxis((codes * scale).reshape(v.shape), -1, axis)


WIDE = False


def mx_kscale(k):
    if not WIDE:
        return np.ones(k)
    levels = np.array([10, -10, 5, -5, 0])
    if k % 512:
        return np.exp2(np.random.permutation(np.resize(levels, k // 32))).repeat(32)
    a = np.empty((k // 512, 16))
    for p in range(k // 512):
        a[p, :8] = np.random.permutation(np.resize(levels, 8))
        for g in range(8):
            far = levels[np.abs(levels - a[p, g]) >= 10]
            a[p, g + 8] = far[np.random.randint(len(far))]
    return np.exp2(a.ravel()).repeat(32)


BF16 = ml_dtypes.bfloat16


def bf(x):
    return np.asarray(x, np.float32).astype(BF16)


def f64(x):
    return np.asarray(x).astype(np.float64)


E2M1 = np.array([0.0, 0.5, 1.0, 1.5, 2.0, 3.0, 4.0, 6.0, -0.0, -0.5, -1.0, -1.5, -2.0, -3.0, -4.0, -6.0])


def pack_weight(w, fmt):
    k, n = w.shape
    w = f64(bf(w)).reshape(k // 32, 32, n)
    amax = np.abs(w).max(1)
    if fmt == "e4m3":
        byte = np.frexp(amax)[1] - 1 + 127 - 7
    else:
        mant, ex = np.frexp(amax / 6.0)
        byte = np.where(mant > 0.5, ex, ex - 1) + 127
    byte = np.clip(np.where(amax > 0, byte, 1), 1, 254)
    scaled = (w * np.exp2(127.0 - byte)[:, None, :]).reshape(k, n).astype(np.float32)
    by_word = np.ascontiguousarray(scaled.reshape(k // 512, 128, 4, n).transpose(0, 1, 3, 2))
    if fmt == "e4m3":
        words = by_word.astype(ml_dtypes.float8_e4m3fn).view(np.uint8)
    else:
        c = by_word.astype(ml_dtypes.float4_e2m1fn).view(np.uint8) & 0xF
        words = c[..., 0::2] | (c[..., 1::2] << 4)
    return np.ascontiguousarray(words), np.ascontiguousarray(byte.astype(np.uint8).reshape(k // 512, 16, n))


def unpack_weight(words, scales, fmt):
    g, p, n, _ = words.shape
    if fmt == "e4m3":
        vals = np.ascontiguousarray(words).view(ml_dtypes.float8_e4m3fn).astype(np.float64)
    else:
        nib = np.empty((g, p, n, 4), np.uint8)
        nib[..., 0::2] = words & 0xF
        nib[..., 1::2] = words >> 4
        vals = E2M1[nib]
    vals = vals * np.repeat(np.exp2(scales.astype(np.float64) - 127.0), 8, axis=1)[..., None]
    return vals.transpose(0, 1, 3, 2).reshape(g * 512, n)
def pack4(w):
    words, scales = pack_weight(w, "e2m1")
    return words.reshape(words.shape[0], 128, -1), scales


def unpack4(words, scales):
    return unpack_weight(words.reshape(words.shape[0], 128, -1, 2), scales, "e2m1")


def planes(Y):
    n, m = Y.shape
    b = f64(bf(Y)).reshape(n // 32, 32, m)
    amax = np.abs(b).max(1)
    byte = np.clip(np.where(amax > 0, np.frexp(amax)[1] - 1 + 127 - 7, 1), 1, 254)
    codes = (b * np.exp2(127.0 - byte)[:, None, :]).reshape(n, m).astype(np.float32).astype(ml_dtypes.float8_e4m3fn).view(np.uint8)
    words = codes.reshape(n // 512, 128, 4, m).transpose(0, 1, 3, 2)
    return np.ascontiguousarray(words), np.ascontiguousarray(byte.astype(np.uint8).reshape(n // 512, 16, m))


N, D, M = 2048, 1024, 1024


def setup_inputs():
    s = mx_kscale(D)
    u = mx_kscale(N)
    x = bf(np.random.standard_normal((N, D)) * s)
    w_words, w_scales = pack4(np.random.standard_normal((D, M)) / np.sqrt(D) / s[:, None])
    return {
        "x": x,
        "w_words": w_words,
        "w_scales": w_scales,
        "c": bf(0.2 * np.random.standard_normal(M)),
        "k": bf(np.random.standard_normal(M)),
        "a": bf((1.0 + 0.3 * np.random.standard_normal(N)) * u),
        "b": bf((1.0 + 0.3 * np.random.standard_normal(N)) / u),
    }


def core(x, w_words, w_scales, c, k, a, b):
    root_n = np.sqrt(x.shape[0])
    w = unpack4(w_words, w_scales)
    y = (mxq(f64(x), 1, "e4m3") @ w) + f64(c)[None, :]
    f = (y + f64(k)[None, :] * np.tanh(y)) * f64(a)[:, None]
    h = y * f64(b)[:, None]
    m = (mxq(f, 0, "e4m3").T @ mxq(h, 0, "e4m3")) / root_n
    return -m + root_n * np.eye(w.shape[1])


def reference(x, w_words, w_scales, c, k, a, b):
    R_out = core(x, w_words, w_scales, c, k, a, b)
    words, scales = planes(R_out)
    return R_out, words, scales

@@ -1,0 +1,427 @@
+import math
+from contextlib import ExitStack
+
+import concourse.mybir as mybir
+from concourse.masks import make_identity
+
+N, D, M = 2048, 1024, 1024
+FLOPS = 2 * N * D * M * 2
+
+F32 = mybir.dt.float32
+BF16 = mybir.dt.bfloat16
+I32 = mybir.dt.int32
+U32 = mybir.dt.uint32
+U8 = mybir.dt.uint8
+FP8X4 = mybir.dt.float8_e4m3fn_x4
+FP4X4 = mybir.dt.float4_e2m1fn_x4
+ADD = mybir.AluOpType.add
+MULT = mybir.AluOpType.mult
+ACT = mybir.ActivationFunctionType
+
+P = 128
+ROOT_N = math.sqrt(N)
+NG = N // 512
+KP = D // 512
+
+
+def tile_extendedinfomaxicarelativegrad_x2_kernel(
+    tc, x, w_words, w_scales, c, k, a, b, out_0, out_1, out_2
+):
+    nc = tc.nc
+    with ExitStack() as ctx:
+        keep = ctx.enter_context(tc.tile_pool(name="keep", bufs=1))
+        work = ctx.enter_context(tc.tile_pool(name="work", bufs=2))
+        psum = ctx.enter_context(tc.psum_pool(name="psum", bufs=1))
+        ctx.enter_context(tc.manual_schedule())
+
+        def bank(tag, bufs, dtype=F32, shape=(P, 512)):
+            return psum.tile(list(shape), dtype, name=tag, tag=tag, bufs=bufs)
+
+        vec = keep.tile([P, 128], BF16, name="vec")
+        warm = keep.tile([P, 2], F32, name="warm")
+        ws = keep.tile([P, KP, M], U8, name="ws", align_bytes=64)
+        wc = keep.tile([P, KP, 2 * M], U8, name="wc", align_bytes=64)
+        nc.vector.memset(warm[:], 0.0)
+        nc.vector.memset(vec[:], 0.0)
+        nc.vector.memset(ws[:].rearrange("p g n -> p (g n)").bitcast(I32), 0)
+
+        xr = []
+        for g in range(NG):
+            t = work.tile([P, 4, D], BF16, name="xr", tag="xr", bufs=4, align_bytes=64)
+            xr.append(t)
+
+        def load_x(g, u):
+            src = x[512 * g : 512 * g + 512, :].rearrange("(p t) d -> p t d", t=4)
+            nc.sync.dma_start(out=xr[g][:, 2 * u : 2 * u + 2, :], in_=src[:, 2 * u : 2 * u + 2, :])
+
+        load_x(0, 0)
+        load_x(0, 1)
+        for (v, r0, nr) in ((c, 0, 8), (k, 8, 8), (a, 16, 16), (b, 32, 16)):
+            nc.scalar.dma_start(out=vec[r0 : r0 + nr, :], in_=v.rearrange("(r n) -> r n", n=128))
+        for q in range(4):
+            nc.scalar.dma_start(
+                out=ws[32 * q : 32 * q + 4, :, :].bitcast(I32),
+                in_=w_scales[:, 4 * q : 4 * q + 4, :].rearrange("g r n -> r g n").bitcast(I32),
+            )
+        nc.scalar.activation(out=warm[:], in_=warm[:], func=ACT.Tanh)
+        for g in range(KP):
+            nc.sync.dma_start(out=wc[:, g, :].bitcast(I32), in_=w_words[g].bitcast(I32))
+        for g in range(1, NG):
+            load_x(g, 0)
+            load_x(g, 1)
+
+        id_b = keep.tile([P, P], BF16, name="id_b")
+        id_f = keep.tile([P, P], F32, name="id_f")
+        root_i = keep.tile([P, P], F32, name="root_i")
+        make_identity(nc, id_f[:])
+        make_identity(nc, id_b[:])
+        nc.gpsimd.tensor_scalar(out=root_i[:], in0=id_f[:], scalar1=ROOT_N, scalar2=0.0, op0=MULT, op1=ADD)
+
+        vt = keep.tile([P, 128], BF16, name="vt")
+        ck = keep.tile([P, 16], F32, name="ck")
+        ab = [keep.tile([P, N], BF16, name="a_bc"), keep.tile([P, N], BF16, name="b_bc")]
+
+        xc = keep.tile([P, KP, N], U32, name="xc", align_bytes=64)
+        xs = keep.tile([P, KP, N], U8, name="xs", align_bytes=64)
+        fc = keep.tile([P, NG, M], U32, name="fc", align_bytes=64)
+        fs = keep.tile([P, NG, M], U8, name="fs", align_bytes=64)
+        hc = keep.tile([P, NG, M], U32, name="hc", align_bytes=64)
+        hs = keep.tile([P, NG, M], U8, name="hs", align_bytes=64)
+        res = [keep.tile([P, 4, M], F32, name="res0"), keep.tile([P, 4, M], F32, name="res1")]
+        oc = [keep.tile([P, M], U32, name="oc0", align_bytes=64), keep.tile([P, M], U32, name="oc1", align_bytes=64)]
+        os_ = [keep.tile([P, M], U8, name="os0", align_bytes=64), keep.tile([P, M], U8, name="os1", align_bytes=64)]
+
+        def vectors_t():
+            pv = bank("y", 4, BF16, (P, 128))
+            nc.tensor.transpose(pv[:], vec[:], id_b[:])
+            nc.vector.tensor_copy(out=vt[:], in_=pv[:])
+            nc.vector.tensor_copy(out=ck[:], in_=vt[:, 0:16])
+
+        def vectors_bc(g, tag, bufs):
+            for which in range(2):
+                pb = bank(tag, bufs, BF16)
+                for i in range(4):
+                    col = 16 + 16 * which + 4 * g + i
+                    nc.tensor.transpose(
+                        pb[:, 128 * i : 128 * i + 128], vt[:, col : col + 1].to_broadcast([P, P]), id_b[:]
+                    )
+                nc.vector.tensor_copy(
+                    out=ab[which][:, 512 * g : 512 * g + 512].rearrange("p (u r e) -> p u r e", u=2, e=2),
+                    in_=pb[:].rearrange("p (r u e) -> p u r e", u=2, e=2),
+                )
+
+        xg = {}
+        xb = {}
+
+        def x_transpose(g, kp, tag="o"):
+            xg[g, kp] = work.tile([P, 512, 4], BF16, name="xg", tag="xg", bufs=3, align_bytes=64)
+            for u in range(2):
+                pb = bank(tag, 2, F32, (P, 4, 128))
+                for e in range(2):
+                    words = xr[g][:, 2 * u + e, :].bitcast(F32)
+                    for j in range(2):
+                        nc.tensor.transpose(
+                            pb[:, 2 * e + j, :], words[:, 256 * kp + j : 256 * kp + 256 : 2], id_f[:]
+                        )
+                xb[g, kp, u] = pb
+
+        def x_copy(g, kp, engines):
+            for u in range(2):
+                dst = xg[g, kp][:, 256 * u : 256 * u + 256, :].rearrange("p q j -> p (q j)").bitcast(F32)
+                dst = dst.rearrange("p (r j) -> p r j", j=4)
+                src = xb[g, kp, u][:].rearrange("p j r -> p r j")
+                if engines[u] == "s":
+                    nc.scalar.copy(out=dst, in_=src)
+                else:
+                    nc.vector.tensor_copy(out=dst, in_=src)
+
+        def x_quant(g, kp):
+            cols = slice(512 * g, 512 * g + 512)
+            nc.vector.quantize_mx(
+                out=xc[:, kp, cols].bitcast(FP8X4),
+                scales=xs[:, kp, cols],
+                in_=xg[g, kp][:].rearrange("p q j -> p (q j)"),
+            )
+
+        steps = [(pr, g) for g in range(NG) for pr in (0, 1)]
+        steps += [(pr, g) for pr in (2, 3) for g in range(NG)]
+        yb, ys, tt, fb, hb, fp, hp, fg, hg = {}, {}, {}, {}, {}, {}, {}, {}, {}
+
+        def stage1(s):
+            pr, g = steps[s]
+            for l in range(2):
+                mt = 2 * pr + l
+                y = bank("y", 4)
+                for kp in range(KP):
+                    nc.tensor.matmul_mx(
+                        out=y[:],
+                        lhsT=wc[:, kp, 256 * mt : 256 * mt + 256].bitcast(FP4X4),
+                        lhsT_scale=ws[:, kp, 128 * mt : 128 * mt + 128],
+                        rhs=xc[:, kp, 512 * g : 512 * g + 512].bitcast(FP8X4),
+                        rhs_scale=xs[:, kp, 512 * g : 512 * g + 512],
+                        start=(kp == 0),
+                        stop=(kp == KP - 1),
+                    )
+                yb[s, l] = y
+
+        by_gpsimd = set(range(2, 16))
+
+        def tanh(s):
+            pr, g = steps[s]
+            for l in range(2):
+                mt = 2 * pr + l
+                t = work.tile([P, 512], F32, name="t", tag="t", bufs=4)
+                nc.scalar.activation(out=t[:], in_=yb[s, l][:], func=ACT.Tanh, bias=ck[:, mt : mt + 1])
+                tt[s, l] = t
+            if pr == 3:
+                ys[s] = work.tile([P, 2, 512], F32, name="ys", tag="xr", bufs=4, align_bytes=64)
+            else:
+                ys[s] = work.tile([P, 2, 512], F32, name="yg", tag="yg", bufs=2)
+            for l in ((1, 0) if pr == 3 else (1,) if s in by_gpsimd else ()):
+                mt = 2 * pr + l
+                nc.scalar.activation(out=ys[s][:, l, :], in_=yb[s, l][:], func=ACT.Identity, bias=ck[:, mt : mt + 1])
+
+        def elementwise(s):
+            pr, g = steps[s]
+            fb[s] = work.tile([P, 2, 512], BF16, name="fb", tag="fb", bufs=3, align_bytes=64)
+            hb[s] = work.tile([P, 2, 512], BF16, name="hb", tag="hb", bufs=5, align_bytes=64)
+            vv = []
+            cols = slice(512 * g, 512 * g + 512)
+
+            def do_v(l):
+                mt = 2 * pr + l
+                v = work.tile([P, 512], F32, name="v", tag="v", bufs=3)
+                nc.vector.scalar_tensor_tensor(
+                    out=v[:], in0=tt[s, l][:], scalar=ck[:, 8 + mt : 9 + mt], in1=yb[s, l][:], op0=MULT, op1=ADD
+                )
+                vv.append(v)
+
+            def do_h(l):
+                mt = 2 * pr + l
+                nc.vector.scalar_tensor_tensor(
+                    out=hb[s][:, l, :], in0=yb[s, l][:], scalar=ck[:, mt : mt + 1], in1=ab[1][:, cols], op0=ADD, op1=MULT
+                )
+
+            def do_f(l):
+                mt = 2 * pr + l
+                nc.vector.scalar_tensor_tensor(
+                    out=fb[s][:, l, :], in0=vv[l][:], scalar=ck[:, mt : mt + 1], in1=ab[0][:, cols], op0=ADD, op1=MULT
+                )
+
+            if s in by_gpsimd:
+                nc.gpsimd.tensor_tensor(out=hb[s][:, 1, :], in0=ys[s][:, 1, :], in1=ab[1][:, cols], op=MULT)
+            do_v(0)
+            do_v(1)
+            if pr < 3:
+                do_h(0)
+            do_f(0)
+            if s not in by_gpsimd:
+                do_h(1)
+            do_f(1)
+
+        def late_h(s):
+            pr, g = steps[s]
+            cols = slice(512 * g, 512 * g + 512)
+            nc.vector.tensor_tensor(out=hb[s][:, 0, :], in0=ys[s][:, 0, :], in1=ab[1][:, cols], op=MULT)
+
+        def transpose(src, dst, s):
+            pb = bank("tr", 2, F32, (P, 2, 2, 128))
+            for u in range(2):
+                for l in range(2):
+                    words = src[s][:, l, :].bitcast(F32)
+                    nc.tensor.transpose(pb[:, u, l, :], words[:, 128 * u : 128 * u + 128], id_f[:])
+            dst[s] = pb
+
+        def f_copy(s):
+            pr, g = steps[s]
+            half, side = pr // 2, pr % 2
+            if side == 0:
+                fg[half, g] = work.tile([P, 512, 4], BF16, name="fg", tag="fg", bufs=5, align_bytes=64)
+            dst = fg[half, g][:].rearrange("p q j -> p (q j)").bitcast(F32)
+            dst = dst.rearrange("p (t r u) -> p t r u", t=4, u=2)[:, :, 64 * side : 64 * side + 64, :]
+            nc.scalar.copy(out=dst, in_=fp[s][:].rearrange("p u l m -> p u (l m)").rearrange("p u (r t) -> p t r u", t=4))
+
+        def h_copy(s):
+            hg[s] = work.tile([P, 256, 4], BF16, name="hg", tag="hg", bufs=3, align_bytes=64)
+            nc.scalar.copy(
+                out=hg[s][:].rearrange("p q j -> p (q j)").bitcast(F32).rearrange("p (m u) -> p m u", u=2),
+                in_=hp[s][:].rearrange("p u l m -> p u (l m)").rearrange("p u m -> p m u"),
+            )
+
+        def h_quant(s):
+            pr, g = steps[s]
+            cols = slice(256 * pr, 256 * pr + 256)
+            nc.vector.quantize_mx(
+                out=hc[:, g, cols].bitcast(FP8X4), scales=hs[:, g, cols], in_=hg[s][:].rearrange("p q j -> p (q j)")
+            )
+
+        def f_quant(s):
+            pr, g = steps[s]
+            half = pr // 2
+            if pr % 2 == 1:
+                cols = slice(512 * half, 512 * half + 512)
+                nc.vector.quantize_mx(
+                    out=fc[:, g, cols].bitcast(FP8X4),
+                    scales=fs[:, g, cols],
+                    in_=fg[half, g][:].rearrange("p q j -> p (q j)"),
+                )
+
+        def stage2(gi, t, j0, n, tag, bufs):
+            rows = slice(512 * gi + 128 * t, 512 * gi + 128 * t + 128)
+            cols = slice(j0, j0 + n)
+            acc = bank(tag, bufs)
+            for g in range(NG):
+                nc.tensor.matmul_mx(
+                    out=acc[:, 0:n],
+                    lhsT=fc[:, g, rows].bitcast(FP8X4),
+                    lhsT_scale=fs[:, g, rows],
+                    rhs=hc[:, g, cols].bitcast(FP8X4),
+                    rhs_scale=hs[:, g, cols],
+                    start=(g == 0),
+                    stop=(g == NG - 1),
+                )
+            return acc
+
+        def result(gi, t, j0, n, acc, engine="s"):
+            dst = res[gi][:, t, j0 : j0 + n]
+            if engine == "s":
+                nc.scalar.activation(out=dst, in_=acc[:, 0:n], func=ACT.Copy, scale=-1.0 / ROOT_N)
+            else:
+                nc.vector.tensor_scalar(
+                    out=dst, in0=acc[:, 0:n], scalar1=-1.0 / ROOT_N, scalar2=None, op0=MULT
+                )
+            if j0 // 512 == gi:
+                q0, q1 = (j0 - 512 * gi) // 4, (j0 + n - 512 * gi) // 4
+                diag = res[gi][:, t, j0 : j0 + n].rearrange("p (q s) -> p q s", s=4)[:, :, t]
+                nc.gpsimd.tensor_tensor(out=diag, in0=diag, in1=root_i[:, q0:q1], op=ADD)
+
+        rb = {}
+
+        def out_cast(gi, j0, n, engine="v"):
+            rb[gi, j0] = work.tile([P, 512, 4], BF16, name="rb", tag="rb", bufs=2, align_bytes=64)
+            dst, src = rb[gi, j0][:, 0:n, :], res[gi][:, :, j0 : j0 + n].rearrange("p t j -> p j t")
+            if engine == "v":
+                nc.vector.tensor_copy(out=dst, in_=src)
+            else:
+                nc.gpsimd.tensor_scalar(out=dst, in0=src, scalar1=1.0, scalar2=0.0, op0=MULT, op1=ADD)
+            dst = out_0[512 * gi : 512 * gi + 512, j0 : j0 + n].rearrange("(p t) j -> p t j", t=4)
+            nc.sync.dma_start(out=dst, in_=res[gi][:, :, j0 : j0 + n])
+
+        def out_quant(gi, j0, n):
+            cols = slice(j0, j0 + n)
+            nc.vector.quantize_mx(
+                out=oc[gi][:, cols].bitcast(FP8X4),
+                scales=os_[gi][:, cols],
+                in_=rb[gi, j0][:, 0:n, :].rearrange("p q j -> p (q j)"),
+            )
+            nc.sync.dma_start(
+                out=out_1[gi, :, cols, :].rearrange("p m t -> p (m t)").bitcast(I32), in_=oc[gi][:, cols].bitcast(I32)
+            )
+
+        def out_scales(gi):
+            for q in range(4):
+                nc.sync.dma_start(
+                    out=out_2[gi, 4 * q : 4 * q + 4, :].bitcast(I32), in_=os_[gi][32 * q : 32 * q + 4, :].bitcast(I32)
+                )
+
+        x_transpose(0, 0)
+        x_copy(0, 0, "sv")
+        x_transpose(0, 1, "tr")
+        x_copy(0, 1, "sv")
+        vectors_t()
+        x_quant(0, 0)
+        x_quant(0, 1)
+        vectors_bc(0, "y", 4)
+        vectors_bc(1, "tr", 2)
+        vectors_bc(2, "o", 2)
+        stage1(0)
+        tanh(0)
+        x_transpose(1, 0)
+        x_copy(1, 0, "ss")
+
+        x_plan = {0: (1, 1), 1: (2, 0), 2: (2, 1), 3: (3, 0), 4: (3, 1)}
+        x_late = {1: (1, 1), 3: (2, 1), 5: (3, 1)}
+        x_early = {0: (1, 0), 2: (2, 0), 4: (3, 0)}
+        n_steps = len(steps)
+        for s in range(n_steps + 1):
+            if s in x_late:
+                x_quant(*x_late[s])
+            if s + 1 < n_steps:
+                stage1(s + 1)
+                tanh(s + 1)
+            if s >= 1:
+                transpose(fb, fp, s - 1)
+                f_copy(s - 1)
+                if s - 1 < 12:
+                    transpose(hb, hp, s - 1)
+                    h_copy(s - 1)
+            if s in x_plan:
+                x_transpose(*x_plan[s])
+                x_copy(*x_plan[s], "ss")
+            if s < n_steps:
+                elementwise(s)
+            if s in x_early:
+                x_quant(*x_early[s])
+            if s == 1:
+                vectors_bc(3, "tr", 2)
+            if s >= 2:
+                if s - 2 < 12:
+                    h_quant(s - 2)
+                f_quant(s - 2)
+            if 10 <= s < 14:
+                t = s - 10
+                result(0, t, 0, 512, stage2(0, t, 0, 512, "o", 2))
+            if s == 14:
+                out_cast(0, 0, 512, "g")
+            if s in (14, 15):
+                for t in (2 * (s - 14), 2 * (s - 14) + 1):
+                    result(0, t, 512, 256, stage2(0, t, 512, 256, "o", 2))
+
+        slots = [0]
+
+        def block_part(gi, t, j0, n, engine):
+            tag, bufs = (("o", 2), ("y", 4), ("y", 4))[slots[0] % 3]
+            slots[0] += 1
+            result(gi, t, j0, n, stage2(gi, t, j0, n, tag, bufs), engine)
+
+        def block(gi, j0, n, engines):
+            for t in range(4):
+                block_part(gi, t, j0, n, engines[t])
+
+        late_h(12)
+        transpose(hb, hp, 12)
+        h_copy(12)
+        late_h(13)
+        transpose(hb, hp, 13)
+        h_copy(13)
+        f_quant(15)
+        late_h(14)
+        late_h(15)
+        h_quant(12)
+        h_quant(13)
+        out_cast(0, 512, 256, "g")
+        block_part(1, 0, 0, 512, "s")
+        transpose(hb, hp, 14)
+        transpose(hb, hp, 15)
+        h_copy(14)
+        h_copy(15)
+        out_quant(0, 0, 512)
+        out_quant(0, 512, 256)
+        h_quant(14)
+        h_quant(15)
+        block_part(1, 1, 0, 512, "v")
+        block_part(1, 2, 0, 512, "s")
+        block_part(1, 3, 0, 512, "v")
+        block(1, 512, 256, "svsv")
+        out_cast(1, 0, 512)
+        out_quant(1, 0, 512)
+        block(1, 768, 256, "vsvs")
+        out_cast(1, 512, 256)
+        out_quant(1, 512, 256)
+        block(0, 768, 256, "vsvs")
+        out_cast(1, 768, 256)
+        out_quant(1, 768, 256)
+        out_scales(1)
+        out_cast(0, 768, 256)
+        out_quant(0, 768, 256)
+        out_scales(0)

@@ -19,6 +19,9 @@ MULT = mybir.AluOpType.mult
 ACT = mybir.ActivationFunctionType
 
 P = 128
+G_PIECE = 512
+BY_G = [(), (), (1,), (1,), (1,), (1,), (1,), (1,), (1,), (0, 1), (1,), (1,), (1,), (1,), (), ()]
+LATE = {s: ((0,) if s >= 12 else ()) for s in range(16)}
 ROOT_N = math.sqrt(N)
 NG = N // 512
 KP = D // 512
@@ -56,19 +59,30 @@ def tile_extendedinfomaxicarelativegrad_x2_kernel(
 
         load_x(0, 0)
         load_x(0, 1)
-        for (v, r0, nr) in ((c, 0, 8), (k, 8, 8), (a, 16, 16), (b, 32, 16)):
-            nc.scalar.dma_start(out=vec[r0 : r0 + nr, :], in_=v.rearrange("(r n) -> r n", n=128))
         for q in range(4):
             nc.scalar.dma_start(
                 out=ws[32 * q : 32 * q + 4, :, :].bitcast(I32),
                 in_=w_scales[:, 4 * q : 4 * q + 4, :].rearrange("g r n -> r g n").bitcast(I32),
             )
+        nc.sync.dma_start(out=wc[:].bitcast(I32), in_=w_words.rearrange("g p n -> p g n").bitcast(I32))
+        for (v, r0, nr) in ((c, 0, 8), (k, 8, 8)):
+            nc.scalar.dma_start(out=vec[r0 : r0 + nr, :], in_=v.rearrange("(r n) -> r n", n=128))
         nc.scalar.activation(out=warm[:], in_=warm[:], func=ACT.Tanh)
-        for g in range(KP):
-            nc.sync.dma_start(out=wc[:, g, :].bitcast(I32), in_=w_words[g].bitcast(I32))
+        raw = []
+        for which in range(2):
+            raw_ab = work.tile([P, N], BF16, name="raw_ab", tag="rb", bufs=2, align_bytes=64)
+            raw.append(raw_ab)
+
+        def load_ab(g):
+            cols = slice(512 * g, 512 * g + 512)
+            for which, vector in ((0, a), (1, b)):
+                nc.sync.dma_start(out=raw[which][:, cols], in_=vector[cols].partition_broadcast(P))
+
+        load_ab(0)
         for g in range(1, NG):
             load_x(g, 0)
             load_x(g, 1)
+            load_ab(g)
 
         id_b = keep.tile([P, P], BF16, name="id_b")
         id_f = keep.tile([P, P], F32, name="id_f")
@@ -89,7 +103,7 @@ def tile_extendedinfomaxicarelativegrad_x2_kernel(
         hs = keep.tile([P, NG, M], U8, name="hs", align_bytes=64)
         res = [keep.tile([P, 4, M], F32, name="res0"), keep.tile([P, 4, M], F32, name="res1")]
         oc = [keep.tile([P, M], U32, name="oc0", align_bytes=64), keep.tile([P, M], U32, name="oc1", align_bytes=64)]
-        os_ = [keep.tile([P, M], U8, name="os0", align_bytes=64), keep.tile([P, M], U8, name="os1", align_bytes=64)]
+        out_s = keep.tile([P, 2, M], U8, name="out_s", align_bytes=64)
 
         def vectors_t():
             pv = bank("y", 4, BF16, (P, 128))
@@ -97,43 +111,34 @@ def tile_extendedinfomaxicarelativegrad_x2_kernel(
             nc.vector.tensor_copy(out=vt[:], in_=pv[:])
             nc.vector.tensor_copy(out=ck[:], in_=vt[:, 0:16])
 
-        def vectors_bc(g, tag, bufs):
+        def spread(g):
             for which in range(2):
-                pb = bank(tag, bufs, BF16)
-                for i in range(4):
-                    col = 16 + 16 * which + 4 * g + i
-                    nc.tensor.transpose(
-                        pb[:, 128 * i : 128 * i + 128], vt[:, col : col + 1].to_broadcast([P, P]), id_b[:]
-                    )
                 nc.vector.tensor_copy(
                     out=ab[which][:, 512 * g : 512 * g + 512].rearrange("p (u r e) -> p u r e", u=2, e=2),
-                    in_=pb[:].rearrange("p (r u e) -> p u r e", u=2, e=2),
+                    in_=raw[which][:, 512 * g : 512 * g + 512].rearrange("p (r u e) -> p u r e", u=2, e=2),
                 )
 
         xg = {}
         xb = {}
 
-        def x_transpose(g, kp, tag="o"):
-            xg[g, kp] = work.tile([P, 512, 4], BF16, name="xg", tag="xg", bufs=3, align_bytes=64)
-            for u in range(2):
-                pb = bank(tag, 2, F32, (P, 4, 128))
-                for e in range(2):
-                    words = xr[g][:, 2 * u + e, :].bitcast(F32)
-                    for j in range(2):
-                        nc.tensor.transpose(
-                            pb[:, 2 * e + j, :], words[:, 256 * kp + j : 256 * kp + 256 : 2], id_f[:]
-                        )
-                xb[g, kp, u] = pb
+        def x_transpose(g, kp, u, tag="o"):
+            if (g, kp) not in xg:
+                xg[g, kp] = work.tile([P, 512, 4], BF16, name="xg", tag="xg", bufs=3, align_bytes=64)
+            pb = bank(tag, 2, F32, (P, 4, 128))
+            for e in range(2):
+                words = xr[g][:, 2 * u + e, :].bitcast(F32)
+                for j in range(2):
+                    nc.tensor.transpose(pb[:, 2 * e + j, :], words[:, 256 * kp + j : 256 * kp + 256 : 2], id_f[:])
+            xb[g, kp, u] = pb
 
-        def x_copy(g, kp, engines):
-            for u in range(2):
-                dst = xg[g, kp][:, 256 * u : 256 * u + 256, :].rearrange("p q j -> p (q j)").bitcast(F32)
-                dst = dst.rearrange("p (r j) -> p r j", j=4)
-                src = xb[g, kp, u][:].rearrange("p j r -> p r j")
-                if engines[u] == "s":
-                    nc.scalar.copy(out=dst, in_=src)
-                else:
-                    nc.vector.tensor_copy(out=dst, in_=src)
+        def x_copy(g, kp, u, engine):
+            dst = xg[g, kp][:, 256 * u : 256 * u + 256, :].rearrange("p q j -> p (q j)").bitcast(F32)
+            dst = dst.rearrange("p (r j) -> p r j", j=4)
+            src = xb[g, kp, u][:].rearrange("p j r -> p r j")
+            if engine == "s":
+                nc.scalar.copy(out=dst, in_=src)
+            else:
+                nc.vector.tensor_copy(out=dst, in_=src)
 
         def x_quant(g, kp):
             cols = slice(512 * g, 512 * g + 512)
@@ -147,9 +152,9 @@ def tile_extendedinfomaxicarelativegrad_x2_kernel(
         steps += [(pr, g) for pr in (2, 3) for g in range(NG)]
         yb, ys, tt, fb, hb, fp, hp, fg, hg = {}, {}, {}, {}, {}, {}, {}, {}, {}
 
-        def stage1(s):
+        def stage1(s, which=(0, 1)):
             pr, g = steps[s]
-            for l in range(2):
+            for l in which:
                 mt = 2 * pr + l
                 y = bank("y", 4)
                 for kp in range(KP):
@@ -164,7 +169,8 @@ def tile_extendedinfomaxicarelativegrad_x2_kernel(
                     )
                 yb[s, l] = y
 
-        by_gpsimd = set(range(2, 16))
+        late = {s: LATE[s] for s in range(16)}
+        by_g = {s: BY_G[s] for s in range(16)}
 
         def tanh(s):
             pr, g = steps[s]
@@ -173,18 +179,20 @@ def tile_extendedinfomaxicarelativegrad_x2_kernel(
                 t = work.tile([P, 512], F32, name="t", tag="t", bufs=4)
                 nc.scalar.activation(out=t[:], in_=yb[s, l][:], func=ACT.Tanh, bias=ck[:, mt : mt + 1])
                 tt[s, l] = t
-            if pr == 3:
-                ys[s] = work.tile([P, 2, 512], F32, name="ys", tag="xr", bufs=4, align_bytes=64)
-            else:
-                ys[s] = work.tile([P, 2, 512], F32, name="yg", tag="yg", bufs=2)
-            for l in ((1, 0) if pr == 3 else (1,) if s in by_gpsimd else ()):
+            for l in range(2):
                 mt = 2 * pr + l
-                nc.scalar.activation(out=ys[s][:, l, :], in_=yb[s, l][:], func=ACT.Identity, bias=ck[:, mt : mt + 1])
+                if l in late[s]:
+                    ys[s, l] = work.tile([P, 512], F32, name="yl", tag="xr", bufs=4, align_bytes=64)
+                elif l in by_g[s]:
+                    ys[s, l] = work.tile([P, 512], F32, name="yg", tag="yg", bufs=2)
+                else:
+                    continue
+                nc.scalar.activation(out=ys[s, l][:], in_=yb[s, l][:], func=ACT.Identity, bias=ck[:, mt : mt + 1])
 
         def elementwise(s):
             pr, g = steps[s]
             fb[s] = work.tile([P, 2, 512], BF16, name="fb", tag="fb", bufs=3, align_bytes=64)
-            hb[s] = work.tile([P, 2, 512], BF16, name="hb", tag="hb", bufs=5, align_bytes=64)
+            hb[s] = work.tile([P, 2, 512], BF16, name="hb", tag="hb", bufs=6, align_bytes=64)
             vv = []
             cols = slice(512 * g, 512 * g + 512)
 
@@ -208,21 +216,29 @@ def tile_extendedinfomaxicarelativegrad_x2_kernel(
                     out=fb[s][:, l, :], in0=vv[l][:], scalar=ck[:, mt : mt + 1], in1=ab[0][:, cols], op0=ADD, op1=MULT
                 )
 
-            if s in by_gpsimd:
-                nc.gpsimd.tensor_tensor(out=hb[s][:, 1, :], in0=ys[s][:, 1, :], in1=ab[1][:, cols], op=MULT)
+            for l in by_g[s]:
+                for i in range(0, 512, G_PIECE):
+                    nc.gpsimd.tensor_tensor(
+                        out=hb[s][:, l, i : i + G_PIECE],
+                        in0=ys[s, l][:, i : i + G_PIECE],
+                        in1=ab[1][:, 512 * g + i : 512 * g + i + G_PIECE],
+                        op=MULT,
+                    )
             do_v(0)
             do_v(1)
-            if pr < 3:
-                do_h(0)
-            do_f(0)
-            if s not in by_gpsimd:
-                do_h(1)
+            for l in range(2):
+                if l == 1:
+                    do_f(0)
+                if l not in by_g[s] and l not in late[s]:
+                    do_h(l)
             do_f(1)
 
         def late_h(s):
-            pr, g = steps[s]
-            cols = slice(512 * g, 512 * g + 512)
-            nc.vector.tensor_tensor(out=hb[s][:, 0, :], in0=ys[s][:, 0, :], in1=ab[1][:, cols], op=MULT)
+            g = steps[s][1]
+            for l in late[s]:
+                nc.vector.tensor_tensor(
+                    out=hb[s][:, l, :], in0=ys[s, l][:], in1=ab[1][:, 512 * g : 512 * g + 512], op=MULT
+                )
 
         def transpose(src, dst, s):
             pb = bank("tr", 2, F32, (P, 2, 2, 128))
@@ -266,11 +282,12 @@ def tile_extendedinfomaxicarelativegrad_x2_kernel(
                     in_=fg[half, g][:].rearrange("p q j -> p (q j)"),
                 )
 
-        def stage2(gi, t, j0, n, tag, bufs):
+        def stage2(gi, t, j0, n, tag, bufs, groups=range(NG), acc=None):
             rows = slice(512 * gi + 128 * t, 512 * gi + 128 * t + 128)
             cols = slice(j0, j0 + n)
-            acc = bank(tag, bufs)
-            for g in range(NG):
+            if acc is None:
+                acc = bank(tag, bufs)
+            for g in groups:
                 nc.tensor.matmul_mx(
                     out=acc[:, 0:n],
                     lhsT=fc[:, g, rows].bitcast(FP8X4),
@@ -302,6 +319,8 @@ def tile_extendedinfomaxicarelativegrad_x2_kernel(
             dst, src = rb[gi, j0][:, 0:n, :], res[gi][:, :, j0 : j0 + n].rearrange("p t j -> p j t")
             if engine == "v":
                 nc.vector.tensor_copy(out=dst, in_=src)
+            elif engine == "s":
+                nc.scalar.copy(out=dst, in_=src)
             else:
                 nc.gpsimd.tensor_scalar(out=dst, in0=src, scalar1=1.0, scalar2=0.0, op0=MULT, op1=ADD)
             dst = out_0[512 * gi : 512 * gi + 512, j0 : j0 + n].rearrange("(p t) j -> p t j", t=4)
@@ -311,33 +330,33 @@ def tile_extendedinfomaxicarelativegrad_x2_kernel(
             cols = slice(j0, j0 + n)
             nc.vector.quantize_mx(
                 out=oc[gi][:, cols].bitcast(FP8X4),
-                scales=os_[gi][:, cols],
+                scales=out_s[:, gi, cols],
                 in_=rb[gi, j0][:, 0:n, :].rearrange("p q j -> p (q j)"),
             )
             nc.sync.dma_start(
                 out=out_1[gi, :, cols, :].rearrange("p m t -> p (m t)").bitcast(I32), in_=oc[gi][:, cols].bitcast(I32)
             )
 
-        def out_scales(gi):
+        def out_scales():
             for q in range(4):
                 nc.sync.dma_start(
-                    out=out_2[gi, 4 * q : 4 * q + 4, :].bitcast(I32), in_=os_[gi][32 * q : 32 * q + 4, :].bitcast(I32)
+                    out=out_2[:, 4 * q : 4 * q + 4, :].rearrange("g r n -> r g n").bitcast(I32),
+                    in_=out_s[32 * q : 32 * q + 4, :, :].bitcast(I32),
                 )
 
-        x_transpose(0, 0)
-        x_copy(0, 0, "sv")
-        x_transpose(0, 1, "tr")
-        x_copy(0, 1, "sv")
+        for (kp, u, tag, engine) in ((0, 0, "o", "s"), (1, 0, "o", "v"), (0, 1, "tr", "s"), (1, 1, "tr", "v")):
+            x_transpose(0, kp, u, tag)
+            x_copy(0, kp, u, engine)
         vectors_t()
         x_quant(0, 0)
         x_quant(0, 1)
-        vectors_bc(0, "y", 4)
-        vectors_bc(1, "tr", 2)
-        vectors_bc(2, "o", 2)
+        spread(0)
         stage1(0)
         tanh(0)
-        x_transpose(1, 0)
-        x_copy(1, 0, "ss")
+        spread(1)
+        for u in range(2):
+            x_transpose(1, 0, u)
+            x_copy(1, 0, u, "s")
 
         x_plan = {0: (1, 1), 1: (2, 0), 2: (2, 1), 3: (3, 0), 4: (3, 1)}
         x_late = {1: (1, 1), 3: (2, 1), 5: (3, 1)}
@@ -346,36 +365,42 @@ def tile_extendedinfomaxicarelativegrad_x2_kernel(
         for s in range(n_steps + 1):
             if s in x_late:
                 x_quant(*x_late[s])
-            if s + 1 < n_steps:
-                stage1(s + 1)
-                tanh(s + 1)
+            more = s + 1 < n_steps
+            if more:
+                stage1(s + 1, (0,))
             if s >= 1:
                 transpose(fb, fp, s - 1)
-                f_copy(s - 1)
-                if s - 1 < 12:
-                    transpose(hb, hp, s - 1)
-                    h_copy(s - 1)
             if s in x_plan:
-                x_transpose(*x_plan[s])
-                x_copy(*x_plan[s], "ss")
+                x_transpose(*x_plan[s], 0)
+            if s in x_plan:
+                x_copy(*x_plan[s], 0, "s")
+                x_transpose(*x_plan[s], 1)
+                x_copy(*x_plan[s], 1, "s")
+            if more:
+                stage1(s + 1, (1,))
+                tanh(s + 1)
+            if s >= 1 and not late[s - 1]:
+                transpose(hb, hp, s - 1)
+            if s >= 1:
+                f_copy(s - 1)
+                if not late[s - 1]:
+                    h_copy(s - 1)
             if s < n_steps:
                 elementwise(s)
             if s in x_early:
                 x_quant(*x_early[s])
-            if s == 1:
-                vectors_bc(3, "tr", 2)
+            if s in (1, 2):
+                spread(s + 1)
             if s >= 2:
-                if s - 2 < 12:
+                if not late[s - 2]:
                     h_quant(s - 2)
                 f_quant(s - 2)
             if 10 <= s < 14:
                 t = s - 10
-                result(0, t, 0, 512, stage2(0, t, 0, 512, "o", 2))
-            if s == 14:
-                out_cast(0, 0, 512, "g")
+                result(0, t, 0, 512, stage2(0, t, 0, 512, "o", 2), "s")
             if s in (14, 15):
                 for t in (2 * (s - 14), 2 * (s - 14) + 1):
-                    result(0, t, 512, 256, stage2(0, t, 512, 256, "o", 2))
+                    result(0, t, 512, 256, stage2(0, t, 512, 256, "o", 2), "s")
 
         slots = [0]
 
@@ -388,40 +413,48 @@ def tile_extendedinfomaxicarelativegrad_x2_kernel(
             for t in range(4):
                 block_part(gi, t, j0, n, engines[t])
 
-        late_h(12)
-        transpose(hb, hp, 12)
-        h_copy(12)
-        late_h(13)
-        transpose(hb, hp, 13)
-        h_copy(13)
+        def late_part(s):
+            late_h(s)
+            transpose(hb, hp, s)
+            h_copy(s)
+
+        early = [stage2(1, t, 0, 512, "o", 2, range(2)) for t in range(2)]
+        late_part(12)
+        for t in range(2):
+            stage2(1, t, 0, 512, "o", 2, range(2, 3), early[t])
+        late_part(13)
         f_quant(15)
+        for t in range(2):
+            stage2(1, t, 0, 512, "o", 2, range(3, 4), early[t])
+            result(1, t, 0, 512, early[t])
         late_h(14)
-        late_h(15)
         h_quant(12)
+        late_h(15)
         h_quant(13)
-        out_cast(0, 512, 256, "g")
-        block_part(1, 0, 0, 512, "s")
         transpose(hb, hp, 14)
-        transpose(hb, hp, 15)
         h_copy(14)
-        h_copy(15)
-        out_quant(0, 0, 512)
-        out_quant(0, 512, 256)
-        h_quant(14)
-        h_quant(15)
-        block_part(1, 1, 0, 512, "v")
         block_part(1, 2, 0, 512, "s")
-        block_part(1, 3, 0, 512, "v")
-        block(1, 512, 256, "svsv")
+        out_cast(0, 0, 512)
+        out_cast(0, 512, 256)
+        out_quant(0, 0, 512)
+        h_quant(14)
+        out_quant(0, 512, 256)
+        transpose(hb, hp, 15)
+        h_copy(15)
+        block_part(1, 3, 0, 512, "s")
+        h_quant(15)
+        block(1, 512, 256, "ssss")
         out_cast(1, 0, 512)
-        out_quant(1, 0, 512)
-        block(1, 768, 256, "vsvs")
+        block(1, 768, 256, "ssss")
         out_cast(1, 512, 256)
+        out_quant(1, 0, 512)
         out_quant(1, 512, 256)
-        block(0, 768, 256, "vsvs")
+        block(0, 768, 128, "ssss")
         out_cast(1, 768, 256)
+        out_cast(0, 768, 128)
         out_quant(1, 768, 256)
-        out_scales(1)
-        out_cast(0, 768, 256)
-        out_quant(0, 768, 256)
-        out_scales(0)
+        out_quant(0, 768, 128)
+        block(0, 896, 128, "svsv")
+        out_cast(0, 896, 128)
+        out_quant(0, 896, 128)
+        out_scales()

@@ -20,7 +20,7 @@ ACT = mybir.ActivationFunctionType
 
 P = 128
 G_PIECE = 512
-BY_G = [(), (), (1,), (1,), (1,), (1,), (1,), (1,), (1,), (0, 1), (1,), (1,), (1,), (1,), (), ()]
+BY_G = [(), (), (), (1,), (), (1,), (1,), (1,), (1,), (1,), (1,), (1,), (1,), (1,), (1,), ()]
 LATE = {s: ((0,) if s >= 12 else ()) for s in range(16)}
 ROOT_N = math.sqrt(N)
 NG = N // 512
@@ -57,6 +57,8 @@ def tile_extendedinfomaxicarelativegrad_x2_kernel(
             src = x[512 * g : 512 * g + 512, :].rearrange("(p t) d -> p t d", t=4)
             nc.sync.dma_start(out=xr[g][:, 2 * u : 2 * u + 2, :], in_=src[:, 2 * u : 2 * u + 2, :])
 
+        for (v, r0, nr) in ((c, 0, 8), (k, 8, 8), (a, 16, 16), (b, 32, 16)):
+            nc.scalar.dma_start(out=vec[r0 : r0 + nr, :], in_=v.rearrange("(r n) -> r n", n=128))
         load_x(0, 0)
         load_x(0, 1)
         for q in range(4):
@@ -65,24 +67,20 @@ def tile_extendedinfomaxicarelativegrad_x2_kernel(
                 in_=w_scales[:, 4 * q : 4 * q + 4, :].rearrange("g r n -> r g n").bitcast(I32),
             )
         nc.sync.dma_start(out=wc[:].bitcast(I32), in_=w_words.rearrange("g p n -> p g n").bitcast(I32))
-        for (v, r0, nr) in ((c, 0, 8), (k, 8, 8)):
-            nc.scalar.dma_start(out=vec[r0 : r0 + nr, :], in_=v.rearrange("(r n) -> r n", n=128))
         nc.scalar.activation(out=warm[:], in_=warm[:], func=ACT.Tanh)
-        raw = []
-        for which in range(2):
-            raw_ab = work.tile([P, N], BF16, name="raw_ab", tag="rb", bufs=2, align_bytes=64)
-            raw.append(raw_ab)
-
-        def load_ab(g):
-            cols = slice(512 * g, 512 * g + 512)
-            for which, vector in ((0, a), (1, b)):
-                nc.sync.dma_start(out=raw[which][:, cols], in_=vector[cols].partition_broadcast(P))
-
-        load_ab(0)
         for g in range(1, NG):
             load_x(g, 0)
             load_x(g, 1)
-            load_ab(g)
+        raw = []
+        for which, vector in ((0, a), (1, b)):
+            raw_ab = work.tile([P, 1024], BF16, name="raw_ab", tag="rb", bufs=2, align_bytes=64)
+            raw.append(raw_ab)
+        for g in (2, 3):
+            for which, vector in ((0, a), (1, b)):
+                cols = slice(512 * g - 1024, 512 * g - 512)
+                nc.sync.dma_start(
+                    out=raw[which][:, cols], in_=vector[512 * g : 512 * g + 512].partition_broadcast(P)
+                )
 
         id_b = keep.tile([P, P], BF16, name="id_b")
         id_f = keep.tile([P, P], F32, name="id_f")
@@ -111,11 +109,27 @@ def tile_extendedinfomaxicarelativegrad_x2_kernel(
             nc.vector.tensor_copy(out=vt[:], in_=pv[:])
             nc.vector.tensor_copy(out=ck[:], in_=vt[:, 0:16])
 
-        def spread(g):
+        def spread(g, tag, engine):
+            pb = bank(tag, 4 if tag == "y" else 2, BF16, (P, 2, 512))
+            for which in range(2):
+                for i in range(4):
+                    col = 16 + 16 * which + 4 * g + i
+                    nc.tensor.transpose(
+                        pb[:, which, 128 * i : 128 * i + 128], vt[:, col : col + 1].to_broadcast([P, P]), id_b[:]
+                    )
+            for which in range(2):
+                dst = ab[which][:, 512 * g : 512 * g + 512].rearrange("p (u r e) -> p u r e", u=2, e=2)
+                src = pb[:, which, :].rearrange("p (r u e) -> p u r e", u=2, e=2)
+                if engine == "s":
+                    nc.scalar.copy(out=dst, in_=src)
+                else:
+                    nc.vector.tensor_copy(out=dst, in_=src)
+
+        def spread_late(g):
             for which in range(2):
                 nc.vector.tensor_copy(
                     out=ab[which][:, 512 * g : 512 * g + 512].rearrange("p (u r e) -> p u r e", u=2, e=2),
-                    in_=raw[which][:, 512 * g : 512 * g + 512].rearrange("p (r u e) -> p u r e", u=2, e=2),
+                    in_=raw[which][:, 512 * g - 1024 : 512 * g - 512].rearrange("p (r u e) -> p u r e", u=2, e=2),
                 )
 
         xg = {}
@@ -140,45 +154,54 @@ def tile_extendedinfomaxicarelativegrad_x2_kernel(
             else:
                 nc.vector.tensor_copy(out=dst, in_=src)
 
-        def x_quant(g, kp):
-            cols = slice(512 * g, 512 * g + 512)
+        def x_quant(g, kp, q0=0, nq=512):
+            cols = slice(512 * g + q0, 512 * g + q0 + nq)
             nc.vector.quantize_mx(
                 out=xc[:, kp, cols].bitcast(FP8X4),
                 scales=xs[:, kp, cols],
-                in_=xg[g, kp][:].rearrange("p q j -> p (q j)"),
+                in_=xg[g, kp][:, q0 : q0 + nq, :].rearrange("p q j -> p (q j)"),
             )
 
         steps = [(pr, g) for g in range(NG) for pr in (0, 1)]
         steps += [(pr, g) for pr in (2, 3) for g in range(NG)]
         yb, ys, tt, fb, hb, fp, hp, fg, hg = {}, {}, {}, {}, {}, {}, {}, {}, {}
 
-        def stage1(s, which=(0, 1)):
+        def pieces(s):
+            return ((0, 256), (256, 256)) if s == 0 else ((0, 512),)
+
+        def stage1(s, l, piece=0):
             pr, g = steps[s]
-            for l in which:
-                mt = 2 * pr + l
-                y = bank("y", 4)
+            mt = 2 * pr + l
+            q0, nq = pieces(s)[piece]
+            if piece == 0:
+                yb[s, l] = bank("y", 4)
+            width = 512 if nq == 512 else 128
+            for q in range(q0, q0 + nq, width):
                 for kp in range(KP):
                     nc.tensor.matmul_mx(
-                        out=y[:],
+                        out=yb[s, l][:, q : q + width],
                         lhsT=wc[:, kp, 256 * mt : 256 * mt + 256].bitcast(FP4X4),
                         lhsT_scale=ws[:, kp, 128 * mt : 128 * mt + 128],
-                        rhs=xc[:, kp, 512 * g : 512 * g + 512].bitcast(FP8X4),
-                        rhs_scale=xs[:, kp, 512 * g : 512 * g + 512],
+                        rhs=xc[:, kp, 512 * g + q : 512 * g + q + width].bitcast(FP8X4),
+                        rhs_scale=xs[:, kp, 512 * g + q : 512 * g + q + width],
                         start=(kp == 0),
                         stop=(kp == KP - 1),
                     )
-                yb[s, l] = y
 
         late = {s: LATE[s] for s in range(16)}
         by_g = {s: BY_G[s] for s in range(16)}
 
-        def tanh(s):
+        def tanh(s, piece=0):
             pr, g = steps[s]
+            q0, nq = pieces(s)[piece]
             for l in range(2):
                 mt = 2 * pr + l
-                t = work.tile([P, 512], F32, name="t", tag="t", bufs=4)
-                nc.scalar.activation(out=t[:], in_=yb[s, l][:], func=ACT.Tanh, bias=ck[:, mt : mt + 1])
-                tt[s, l] = t
+                if piece == 0:
+                    t = work.tile([P, 512], F32, name="t", tag="t", bufs=4)
+                    tt[s, l] = t
+                nc.scalar.activation(
+                    out=tt[s, l][:, q0 : q0 + nq], in_=yb[s, l][:, q0 : q0 + nq], func=ACT.Tanh, bias=ck[:, mt : mt + 1]
+                )
             for l in range(2):
                 mt = 2 * pr + l
                 if l in late[s]:
@@ -194,28 +217,9 @@ def tile_extendedinfomaxicarelativegrad_x2_kernel(
             fb[s] = work.tile([P, 2, 512], BF16, name="fb", tag="fb", bufs=3, align_bytes=64)
             hb[s] = work.tile([P, 2, 512], BF16, name="hb", tag="hb", bufs=6, align_bytes=64)
             vv = []
-            cols = slice(512 * g, 512 * g + 512)
-
-            def do_v(l):
-                mt = 2 * pr + l
+            for l in range(2):
                 v = work.tile([P, 512], F32, name="v", tag="v", bufs=3)
-                nc.vector.scalar_tensor_tensor(
-                    out=v[:], in0=tt[s, l][:], scalar=ck[:, 8 + mt : 9 + mt], in1=yb[s, l][:], op0=MULT, op1=ADD
-                )
                 vv.append(v)
-
-            def do_h(l):
-                mt = 2 * pr + l
-                nc.vector.scalar_tensor_tensor(
-                    out=hb[s][:, l, :], in0=yb[s, l][:], scalar=ck[:, mt : mt + 1], in1=ab[1][:, cols], op0=ADD, op1=MULT
-                )
-
-            def do_f(l):
-                mt = 2 * pr + l
-                nc.vector.scalar_tensor_tensor(
-                    out=fb[s][:, l, :], in0=vv[l][:], scalar=ck[:, mt : mt + 1], in1=ab[0][:, cols], op0=ADD, op1=MULT
-                )
-
             for l in by_g[s]:
                 for i in range(0, 512, G_PIECE):
                     nc.gpsimd.tensor_tensor(
@@ -224,14 +228,35 @@ def tile_extendedinfomaxicarelativegrad_x2_kernel(
                         in1=ab[1][:, 512 * g + i : 512 * g + i + G_PIECE],
                         op=MULT,
                     )
-            do_v(0)
-            do_v(1)
-            for l in range(2):
-                if l == 1:
-                    do_f(0)
-                if l not in by_g[s] and l not in late[s]:
-                    do_h(l)
-            do_f(1)
+
+            def do_v(l, q0, nq):
+                mt = 2 * pr + l
+                q = slice(q0, q0 + nq)
+                nc.vector.scalar_tensor_tensor(
+                    out=vv[l][:, q], in0=tt[s, l][:, q], scalar=ck[:, 8 + mt : 9 + mt], in1=yb[s, l][:, q], op0=MULT, op1=ADD
+                )
+
+            def times(dst, src, which, l, q0, nq):
+                mt = 2 * pr + l
+                q = slice(q0, q0 + nq)
+                nc.vector.scalar_tensor_tensor(
+                    out=dst[s][:, l, q],
+                    in0=src[:, q],
+                    scalar=ck[:, mt : mt + 1],
+                    in1=ab[which][:, 512 * g + q0 : 512 * g + q0 + nq],
+                    op0=ADD,
+                    op1=MULT,
+                )
+
+            for (q0, nq) in pieces(s):
+                do_v(0, q0, nq)
+                do_v(1, q0, nq)
+                for l in range(2):
+                    if l == 1:
+                        times(fb, vv[0], 0, 0, q0, nq)
+                    if l not in by_g[s] and l not in late[s]:
+                        times(hb, yb[s, l], 1, l, q0, nq)
+                times(fb, vv[1], 0, 1, q0, nq)
 
         def late_h(s):
             g = steps[s][1]
@@ -344,16 +369,20 @@ def tile_extendedinfomaxicarelativegrad_x2_kernel(
                     in_=out_s[32 * q : 32 * q + 4, :, :].bitcast(I32),
                 )
 
-        for (kp, u, tag, engine) in ((0, 0, "o", "s"), (1, 0, "o", "v"), (0, 1, "tr", "s"), (1, 1, "tr", "v")):
-            x_transpose(0, kp, u, tag)
-            x_copy(0, kp, u, engine)
-        vectors_t()
-        x_quant(0, 0)
-        x_quant(0, 1)
-        spread(0)
-        stage1(0)
-        tanh(0)
-        spread(1)
+        for u, tag in ((0, "o"), (1, "tr")):
+            for kp, engine in ((0, "s"), (1, "v")):
+                x_transpose(0, kp, u, tag)
+                x_copy(0, kp, u, engine)
+            if u == 0:
+                vectors_t()
+            for kp in range(KP):
+                x_quant(0, kp, 256 * u, 256)
+        for piece in range(2):
+            for l in range(2):
+                stage1(0, l, piece)
+            tanh(0, piece)
+            if piece == 0:
+                spread(0, "tr", "s")
         for u in range(2):
             x_transpose(1, 0, u)
             x_copy(1, 0, u, "s")
@@ -367,7 +396,7 @@ def tile_extendedinfomaxicarelativegrad_x2_kernel(
                 x_quant(*x_late[s])
             more = s + 1 < n_steps
             if more:
-                stage1(s + 1, (0,))
+                stage1(s + 1, 0)
             if s >= 1:
                 transpose(fb, fp, s - 1)
             if s in x_plan:
@@ -377,10 +406,12 @@ def tile_extendedinfomaxicarelativegrad_x2_kernel(
                 x_transpose(*x_plan[s], 1)
                 x_copy(*x_plan[s], 1, "s")
             if more:
-                stage1(s + 1, (1,))
+                stage1(s + 1, 1)
                 tanh(s + 1)
             if s >= 1 and not late[s - 1]:
                 transpose(hb, hp, s - 1)
+            if s == 0:
+                spread(1, "tr", "s")
             if s >= 1:
                 f_copy(s - 1)
                 if not late[s - 1]:
@@ -389,8 +420,8 @@ def tile_extendedinfomaxicarelativegrad_x2_kernel(
                 elementwise(s)
             if s in x_early:
                 x_quant(*x_early[s])
-            if s in (1, 2):
-                spread(s + 1)
+            if s in (3, 5):
+                spread_late((s + 1) // 2)
             if s >= 2:
                 if not late[s - 2]:
                     h_quant(s - 2)
@@ -443,18 +474,18 @@ def tile_extendedinfomaxicarelativegrad_x2_kernel(
         h_copy(15)
         block_part(1, 3, 0, 512, "s")
         h_quant(15)
-        block(1, 512, 256, "ssss")
+        block(1, 512, 256, "vvvv")
         out_cast(1, 0, 512)
-        block(1, 768, 256, "ssss")
+        block(1, 768, 256, "svsv")
         out_cast(1, 512, 256)
         out_quant(1, 0, 512)
         out_quant(1, 512, 256)
-        block(0, 768, 128, "ssss")
+        block(0, 768, 128, "sssv")
         out_cast(1, 768, 256)
         out_cast(0, 768, 128)
         out_quant(1, 768, 256)
         out_quant(0, 768, 128)
-        block(0, 896, 128, "svsv")
+        block(0, 896, 128, "sssv")
         out_cast(0, 896, 128)
         out_quant(0, 896, 128)
         out_scales()

@@ -20,7 +20,7 @@ ACT = mybir.ActivationFunctionType
 
 P = 128
 G_PIECE = 512
-BY_G = [(), (), (), (1,), (), (1,), (1,), (1,), (1,), (1,), (1,), (1,), (1,), (1,), (1,), ()]
+BY_G = [(), (1,), (), (1,), (1,), (1,), (1,), (1,), (1,), (1,), (1,), (1,), (1,), (1,), (), ()]
 LATE = {s: ((0,) if s >= 12 else ()) for s in range(16)}
 ROOT_N = math.sqrt(N)
 NG = N // 512
@@ -249,14 +249,14 @@ def tile_extendedinfomaxicarelativegrad_x2_kernel(
                 )
 
             for (q0, nq) in pieces(s):
-                do_v(0, q0, nq)
-                do_v(1, q0, nq)
-                for l in range(2):
-                    if l == 1:
-                        times(fb, vv[0], 0, 0, q0, nq)
-                    if l not in by_g[s] and l not in late[s]:
+                for op in "h0 h1 v0 v1 f0 f1".split():
+                    l = int(op[1])
+                    if op[0] == "v":
+                        do_v(l, q0, nq)
+                    elif op[0] == "f":
+                        times(fb, vv[l], 0, l, q0, nq)
+                    elif l not in by_g[s] and l not in late[s]:
                         times(hb, yb[s, l], 1, l, q0, nq)
-                times(fb, vv[1], 0, 1, q0, nq)
 
         def late_h(s):
             g = steps[s][1]
@@ -382,7 +382,7 @@ def tile_extendedinfomaxicarelativegrad_x2_kernel(
                 stage1(0, l, piece)
             tanh(0, piece)
             if piece == 0:
-                spread(0, "tr", "s")
+                spread(0, "tr", "v")
         for u in range(2):
             x_transpose(1, 0, u)
             x_copy(1, 0, u, "s")
@@ -392,40 +392,43 @@ def tile_extendedinfomaxicarelativegrad_x2_kernel(
         x_early = {0: (1, 0), 2: (2, 0), 4: (3, 0)}
         n_steps = len(steps)
         for s in range(n_steps + 1):
+            more = s + 1 < n_steps
             if s in x_late:
                 x_quant(*x_late[s])
-            more = s + 1 < n_steps
             if more:
                 stage1(s + 1, 0)
-            if s >= 1:
-                transpose(fb, fp, s - 1)
             if s in x_plan:
                 x_transpose(*x_plan[s], 0)
             if s in x_plan:
                 x_copy(*x_plan[s], 0, "s")
+            if s in x_plan:
                 x_transpose(*x_plan[s], 1)
-                x_copy(*x_plan[s], 1, "s")
+            if s >= 1:
+                transpose(fb, fp, s - 1)
             if more:
                 stage1(s + 1, 1)
-                tanh(s + 1)
-            if s >= 1 and not late[s - 1]:
-                transpose(hb, hp, s - 1)
-            if s == 0:
-                spread(1, "tr", "s")
-            if s >= 1:
-                f_copy(s - 1)
-                if not late[s - 1]:
-                    h_copy(s - 1)
-            if s < n_steps:
-                elementwise(s)
-            if s in x_early:
-                x_quant(*x_early[s])
             if s in (3, 5):
                 spread_late((s + 1) // 2)
+            if s >= 1 and not late[s - 1]:
+                transpose(hb, hp, s - 1)
+            if s in x_plan:
+                x_copy(*x_plan[s], 1, "s")
+            if more:
+                tanh(s + 1)
+            if s == 0:
+                spread(1, "tr", "s")
+            if s < n_steps:
+                elementwise(s)
             if s >= 2:
-                if not late[s - 2]:
-                    h_quant(s - 2)
                 f_quant(s - 2)
+            if s >= 1:
+                f_copy(s - 1)
+            if s >= 2 and not late[s - 2]:
+                h_quant(s - 2)
+            if s >= 1 and not late[s - 1]:
+                h_copy(s - 1)
+            if s in x_early:
+                x_quant(*x_early[s])
             if 10 <= s < 14:
                 t = s - 10
                 result(0, t, 0, 512, stage2(0, t, 0, 512, "o", 2), "s")
@@ -449,43 +452,67 @@ def tile_extendedinfomaxicarelativegrad_x2_kernel(
             transpose(hb, hp, s)
             h_copy(s)
 
-        early = [stage2(1, t, 0, 512, "o", 2, range(2)) for t in range(2)]
-        late_part(12)
-        for t in range(2):
-            stage2(1, t, 0, 512, "o", 2, range(2, 3), early[t])
-        late_part(13)
-        f_quant(15)
-        for t in range(2):
-            stage2(1, t, 0, 512, "o", 2, range(3, 4), early[t])
-            result(1, t, 0, 512, early[t])
+        late_h(12)
+        acc0 = stage2(1, 0, 0, 512, "o", 2, range(2))
+        acc1 = stage2(1, 1, 0, 512, "o", 2, range(2))
+        acc2 = stage2(1, 2, 0, 512, "y", 4, range(2))
+        late_h(13)
+        transpose(hb, hp, 12)
         late_h(14)
-        h_quant(12)
+        h_copy(12)
+        transpose(hb, hp, 13)
+        stage2(1, 0, 0, 512, "o", 2, range(2, 3), acc0)
+        f_quant(15)
         late_h(15)
-        h_quant(13)
+        acc3 = stage2(1, 3, 0, 512, "y", 4, range(2))
+        stage2(1, 0, 0, 512, "o", 2, range(3, 4), acc0)
         transpose(hb, hp, 14)
-        h_copy(14)
-        block_part(1, 2, 0, 512, "s")
-        out_cast(0, 0, 512)
-        out_cast(0, 512, 256)
+        h_quant(12)
+        out_cast(0, 0, 512, "v")
+        h_copy(13)
         out_quant(0, 0, 512)
-        h_quant(14)
-        out_quant(0, 512, 256)
+        out_cast(0, 512, 256, "v")
         transpose(hb, hp, 15)
+        stage2(1, 2, 0, 512, "o", 2, range(2, 3), acc2)
+        h_copy(14)
+        stage2(1, 2, 0, 512, "o", 2, range(3, 4), acc2)
+        stage2(1, 1, 0, 512, "o", 2, range(2, 3), acc1)
+        result(1, 0, 0, 512, acc0, "s")
+        stage2(1, 3, 0, 512, "o", 2, range(2, 3), acc3)
         h_copy(15)
-        block_part(1, 3, 0, 512, "s")
+        result(1, 2, 0, 512, acc2, "v")
+        h_quant(14)
+        stage2(1, 3, 0, 512, "o", 2, range(3, 4), acc3)
+        stage2(1, 1, 0, 512, "o", 2, range(3, 4), acc1)
+        result(1, 1, 0, 512, acc1, "s")
+        result(1, 3, 0, 512, acc3, "s")
+        h_quant(13)
         h_quant(15)
-        block(1, 512, 256, "vvvv")
-        out_cast(1, 0, 512)
-        block(1, 768, 256, "svsv")
-        out_cast(1, 512, 256)
+        block_part(1, 0, 512, 256, "s")
+        out_quant(0, 512, 256)
+        block_part(1, 1, 512, 256, "v")
+        block_part(1, 2, 512, 256, "v")
+        block_part(1, 3, 512, 256, "v")
+        out_cast(1, 0, 512, "s")
+        out_cast(1, 512, 256, "s")
+        block_part(1, 0, 768, 256, "v")
+        block_part(1, 1, 768, 256, "v")
+        block_part(1, 2, 768, 256, "v")
         out_quant(1, 0, 512)
+        block_part(1, 3, 768, 256, "s")
+        block_part(0, 0, 768, 128, "s")
         out_quant(1, 512, 256)
-        block(0, 768, 128, "sssv")
-        out_cast(1, 768, 256)
-        out_cast(0, 768, 128)
-        out_quant(1, 768, 256)
+        block_part(0, 1, 768, 128, "v")
+        block_part(0, 2, 768, 128, "v")
+        block_part(0, 3, 768, 128, "s")
+        out_cast(0, 768, 128, "v")
         out_quant(0, 768, 128)
-        block(0, 896, 128, "sssv")
-        out_cast(0, 896, 128)
+        block_part(0, 0, 896, 128, "v")
+        block_part(0, 1, 896, 128, "s")
+        out_cast(1, 768, 256, "v")
+        block_part(0, 2, 896, 128, "s")
+        out_quant(1, 768, 256)
+        block_part(0, 3, 896, 128, "s")
+        out_cast(0, 896, 128, "v")
         out_quant(0, 896, 128)
         out_scales()

import math
from contextlib import ExitStack

import concourse.mybir as mybir
from concourse.masks import make_identity

N, D, M = 2048, 1024, 1024
FLOPS = 2 * N * D * M * 2

F32 = mybir.dt.float32
BF16 = mybir.dt.bfloat16
I32 = mybir.dt.int32
U32 = mybir.dt.uint32
U8 = mybir.dt.uint8
FP8X4 = mybir.dt.float8_e4m3fn_x4
FP4X4 = mybir.dt.float4_e2m1fn_x4
ADD = mybir.AluOpType.add
MULT = mybir.AluOpType.mult
ACT = mybir.ActivationFunctionType

P = 128
G_PIECE = 512
BY_G = [(), (1,), (), (1,), (1,), (1,), (1,), (1,), (1,), (1,), (1,), (1,), (1,), (1,), (), ()]
LATE = {s: ((0,) if s >= 12 else ()) for s in range(16)}
ROOT_N = math.sqrt(N)
NG = N // 512
KP = D // 512


def tile_extendedinfomaxicarelativegrad_x2_kernel(
    tc, x, w_words, w_scales, c, k, a, b, out_0, out_1, out_2
):
    nc = tc.nc
    with ExitStack() as ctx:
        keep = ctx.enter_context(tc.tile_pool(name="keep", bufs=1))
        work = ctx.enter_context(tc.tile_pool(name="work", bufs=2))
        psum = ctx.enter_context(tc.psum_pool(name="psum", bufs=1))
        ctx.enter_context(tc.manual_schedule())

        def bank(tag, bufs, dtype=F32, shape=(P, 512)):
            return psum.tile(list(shape), dtype, name=tag, tag=tag, bufs=bufs)

        vec = keep.tile([P, 128], BF16, name="vec")
        warm = keep.tile([P, 2], F32, name="warm")
        ws = keep.tile([P, KP, M], U8, name="ws", align_bytes=64)
        wc = keep.tile([P, KP, 2 * M], U8, name="wc", align_bytes=64)
        nc.vector.memset(warm[:], 0.0)
        nc.vector.memset(vec[:], 0.0)
        nc.vector.memset(ws[:].rearrange("p g n -> p (g n)").bitcast(I32), 0)

        xr = []
        for g in range(NG):
            t = work.tile([P, 4, D], BF16, name="xr", tag="xr", bufs=4, align_bytes=64)
            xr.append(t)

        def load_x(g, u):
            src = x[512 * g : 512 * g + 512, :].rearrange("(p t) d -> p t d", t=4)
            nc.sync.dma_start(out=xr[g][:, 2 * u : 2 * u + 2, :], in_=src[:, 2 * u : 2 * u + 2, :])

        for (v, r0, nr) in ((c, 0, 8), (k, 8, 8), (a, 16, 16), (b, 32, 16)):
            nc.scalar.dma_start(out=vec[r0 : r0 + nr, :], in_=v.rearrange("(r n) -> r n", n=128))
        load_x(0, 0)
        load_x(0, 1)
        for q in range(4):
            nc.scalar.dma_start(
                out=ws[32 * q : 32 * q + 4, :, :].bitcast(I32),
                in_=w_scales[:, 4 * q : 4 * q + 4, :].rearrange("g r n -> r g n").bitcast(I32),
            )
        nc.sync.dma_start(out=wc[:].bitcast(I32), in_=w_words.rearrange("g p n -> p g n").bitcast(I32))
        nc.scalar.activation(out=warm[:], in_=warm[:], func=ACT.Tanh)
        for g in range(1, NG):
            load_x(g, 0)
            load_x(g, 1)
        raw = []
        for which, vector in ((0, a), (1, b)):
            raw_ab = work.tile([P, 1024], BF16, name="raw_ab", tag="rb", bufs=2, align_bytes=64)
            raw.append(raw_ab)
        for g in (2, 3):
            for which, vector in ((0, a), (1, b)):
                cols = slice(512 * g - 1024, 512 * g - 512)
                nc.sync.dma_start(
                    out=raw[which][:, cols], in_=vector[512 * g : 512 * g + 512].partition_broadcast(P)
                )

        id_b = keep.tile([P, P], BF16, name="id_b")
        id_f = keep.tile([P, P], F32, name="id_f")
        root_i = keep.tile([P, P], F32, name="root_i")
        make_identity(nc, id_f[:])
        make_identity(nc, id_b[:])
        nc.gpsimd.tensor_scalar(out=root_i[:], in0=id_f[:], scalar1=ROOT_N, scalar2=0.0, op0=MULT, op1=ADD)

        vt = keep.tile([P, 128], BF16, name="vt")
        ck = keep.tile([P, 16], F32, name="ck")
        ab = [keep.tile([P, N], BF16, name="a_bc"), keep.tile([P, N], BF16, name="b_bc")]

        xc = keep.tile([P, KP, N], U32, name="xc", align_bytes=64)
        xs = keep.tile([P, KP, N], U8, name="xs", align_bytes=64)
        fc = keep.tile([P, NG, M], U32, name="fc", align_bytes=64)
        fs = keep.tile([P, NG, M], U8, name="fs", align_bytes=64)
        hc = keep.tile([P, NG, M], U32, name="hc", align_bytes=64)
        hs = keep.tile([P, NG, M], U8, name="hs", align_bytes=64)
        res = [keep.tile([P, 4, M], F32, name="res0"), keep.tile([P, 4, M], F32, name="res1")]
        oc = [keep.tile([P, M], U32, name="oc0", align_bytes=64), keep.tile([P, M], U32, name="oc1", align_bytes=64)]
        out_s = keep.tile([P, 2, M], U8, name="out_s", align_bytes=64)

        def vectors_t():
            pv = bank("y", 4, BF16, (P, 128))
            nc.tensor.transpose(pv[:], vec[:], id_b[:])
            nc.vector.tensor_copy(out=vt[:], in_=pv[:])
            nc.vector.tensor_copy(out=ck[:], in_=vt[:, 0:16])

        def spread(g, tag, engine):
            pb = bank(tag, 4 if tag == "y" else 2, BF16, (P, 2, 512))
            for which in range(2):
                for i in range(4):
                    col = 16 + 16 * which + 4 * g + i
                    nc.tensor.transpose(
                        pb[:, which, 128 * i : 128 * i + 128], vt[:, col : col + 1].to_broadcast([P, P]), id_b[:]
                    )
            for which in range(2):
                dst = ab[which][:, 512 * g : 512 * g + 512].rearrange("p (u r e) -> p u r e", u=2, e=2)
                src = pb[:, which, :].rearrange("p (r u e) -> p u r e", u=2, e=2)
                if engine == "s":
                    nc.scalar.copy(out=dst, in_=src)
                else:
                    nc.vector.tensor_copy(out=dst, in_=src)

        def spread_late(g):
            for which in range(2):
                nc.vector.tensor_copy(
                    out=ab[which][:, 512 * g : 512 * g + 512].rearrange("p (u r e) -> p u r e", u=2, e=2),
                    in_=raw[which][:, 512 * g - 1024 : 512 * g - 512].rearrange("p (r u e) -> p u r e", u=2, e=2),
                )

        xg = {}
        xb = {}

        def x_transpose(g, kp, u, tag="o"):
            if (g, kp) not in xg:
                xg[g, kp] = work.tile([P, 512, 4], BF16, name="xg", tag="xg", bufs=3, align_bytes=64)
            pb = bank(tag, 2, F32, (P, 4, 128))
            for e in range(2):
                words = xr[g][:, 2 * u + e, :].bitcast(F32)
                for j in range(2):
                    nc.tensor.transpose(pb[:, 2 * e + j, :], words[:, 256 * kp + j : 256 * kp + 256 : 2], id_f[:])
            xb[g, kp, u] = pb

        def x_copy(g, kp, u, engine):
            dst = xg[g, kp][:, 256 * u : 256 * u + 256, :].rearrange("p q j -> p (q j)").bitcast(F32)
            dst = dst.rearrange("p (r j) -> p r j", j=4)
            src = xb[g, kp, u][:].rearrange("p j r -> p r j")
            if engine == "s":
                nc.scalar.copy(out=dst, in_=src)
            else:
                nc.vector.tensor_copy(out=dst, in_=src)

        def x_quant(g, kp, q0=0, nq=512):
            cols = slice(512 * g + q0, 512 * g + q0 + nq)
            nc.vector.quantize_mx(
                out=xc[:, kp, cols].bitcast(FP8X4),
                scales=xs[:, kp, cols],
                in_=xg[g, kp][:, q0 : q0 + nq, :].rearrange("p q j -> p (q j)"),
            )

        steps = [(pr, g) for g in range(NG) for pr in (0, 1)]
        steps += [(pr, g) for pr in (2, 3) for g in range(NG)]
        yb, ys, tt, fb, hb, fp, hp, fg, hg = {}, {}, {}, {}, {}, {}, {}, {}, {}

        def pieces(s):
            return ((0, 256), (256, 256)) if s == 0 else ((0, 512),)

        def stage1(s, l, piece=0):
            pr, g = steps[s]
            mt = 2 * pr + l
            q0, nq = pieces(s)[piece]
            if piece == 0:
                yb[s, l] = bank("y", 4)
            width = 512 if nq == 512 else 128
            for q in range(q0, q0 + nq, width):
                for kp in range(KP):
                    nc.tensor.matmul_mx(
                        out=yb[s, l][:, q : q + width],
                        lhsT=wc[:, kp, 256 * mt : 256 * mt + 256].bitcast(FP4X4),
                        lhsT_scale=ws[:, kp, 128 * mt : 128 * mt + 128],
                        rhs=xc[:, kp, 512 * g + q : 512 * g + q + width].bitcast(FP8X4),
                        rhs_scale=xs[:, kp, 512 * g + q : 512 * g + q + width],
                        start=(kp == 0),
                        stop=(kp == KP - 1),
                    )

        late = {s: LATE[s] for s in range(16)}
        by_g = {s: BY_G[s] for s in range(16)}

        def tanh(s, piece=0):
            pr, g = steps[s]
            q0, nq = pieces(s)[piece]
            for l in range(2):
                mt = 2 * pr + l
                if piece == 0:
                    t = work.tile([P, 512], F32, name="t", tag="t", bufs=4)
                    tt[s, l] = t
                nc.scalar.activation(
                    out=tt[s, l][:, q0 : q0 + nq], in_=yb[s, l][:, q0 : q0 + nq], func=ACT.Tanh, bias=ck[:, mt : mt + 1]
                )
            for l in range(2):
                mt = 2 * pr + l
                if l in late[s]:
                    ys[s, l] = work.tile([P, 512], F32, name="yl", tag="xr", bufs=4, align_bytes=64)
                elif l in by_g[s]:
                    ys[s, l] = work.tile([P, 512], F32, name="yg", tag="yg", bufs=2)
                else:
                    continue
                nc.scalar.activation(out=ys[s, l][:], in_=yb[s, l][:], func=ACT.Identity, bias=ck[:, mt : mt + 1])

        def elementwise(s):
            pr, g = steps[s]
            fb[s] = work.tile([P, 2, 512], BF16, name="fb", tag="fb", bufs=3, align_bytes=64)
            hb[s] = work.tile([P, 2, 512], BF16, name="hb", tag="hb", bufs=6, align_bytes=64)
            vv = []
            for l in range(2):
                v = work.tile([P, 512], F32, name="v", tag="v", bufs=3)
                vv.append(v)
            for l in by_g[s]:
                for i in range(0, 512, G_PIECE):
                    nc.gpsimd.tensor_tensor(
                        out=hb[s][:, l, i : i + G_PIECE],
                        in0=ys[s, l][:, i : i + G_PIECE],
                        in1=ab[1][:, 512 * g + i : 512 * g + i + G_PIECE],
                        op=MULT,
                    )

            def do_v(l, q0, nq):
                mt = 2 * pr + l
                q = slice(q0, q0 + nq)
                nc.vector.scalar_tensor_tensor(
                    out=vv[l][:, q], in0=tt[s, l][:, q], scalar=ck[:, 8 + mt : 9 + mt], in1=yb[s, l][:, q], op0=MULT, op1=ADD
                )

            def times(dst, src, which, l, q0, nq):
                mt = 2 * pr + l
                q = slice(q0, q0 + nq)
                nc.vector.scalar_tensor_tensor(
                    out=dst[s][:, l, q],
                    in0=src[:, q],
                    scalar=ck[:, mt : mt + 1],
                    in1=ab[which][:, 512 * g + q0 : 512 * g + q0 + nq],
                    op0=ADD,
                    op1=MULT,
                )

            for (q0, nq) in pieces(s):
                for op in "h0 h1 v0 v1 f0 f1".split():
                    l = int(op[1])
                    if op[0] == "v":
                        do_v(l, q0, nq)
                    elif op[0] == "f":
                        times(fb, vv[l], 0, l, q0, nq)
                    elif l not in by_g[s] and l not in late[s]:
                        times(hb, yb[s, l], 1, l, q0, nq)

        def late_h(s):
            g = steps[s][1]
            for l in late[s]:
                nc.vector.tensor_tensor(
                    out=hb[s][:, l, :], in0=ys[s, l][:], in1=ab[1][:, 512 * g : 512 * g + 512], op=MULT
                )

        def transpose(src, dst, s):
            pb = bank("tr", 2, F32, (P, 2, 2, 128))
            for u in range(2):
                for l in range(2):
                    words = src[s][:, l, :].bitcast(F32)
                    nc.tensor.transpose(pb[:, u, l, :], words[:, 128 * u : 128 * u + 128], id_f[:])
            dst[s] = pb

        def f_copy(s):
            pr, g = steps[s]
            half, side = pr // 2, pr % 2
            if side == 0:
                fg[half, g] = work.tile([P, 512, 4], BF16, name="fg", tag="fg", bufs=5, align_bytes=64)
            dst = fg[half, g][:].rearrange("p q j -> p (q j)").bitcast(F32)
            dst = dst.rearrange("p (t r u) -> p t r u", t=4, u=2)[:, :, 64 * side : 64 * side + 64, :]
            nc.scalar.copy(out=dst, in_=fp[s][:].rearrange("p u l m -> p u (l m)").rearrange("p u (r t) -> p t r u", t=4))

        def h_copy(s):
            hg[s] = work.tile([P, 256, 4], BF16, name="hg", tag="hg", bufs=3, align_bytes=64)
            nc.scalar.copy(
                out=hg[s][:].rearrange("p q j -> p (q j)").bitcast(F32).rearrange("p (m u) -> p m u", u=2),
                in_=hp[s][:].rearrange("p u l m -> p u (l m)").rearrange("p u m -> p m u"),
            )

        def h_quant(s):
            pr, g = steps[s]
            cols = slice(256 * pr, 256 * pr + 256)
            nc.vector.quantize_mx(
                out=hc[:, g, cols].bitcast(FP8X4), scales=hs[:, g, cols], in_=hg[s][:].rearrange("p q j -> p (q j)")
            )

        def f_quant(s):
            pr, g = steps[s]
            half = pr // 2
            if pr % 2 == 1:
                cols = slice(512 * half, 512 * half + 512)
                nc.vector.quantize_mx(
                    out=fc[:, g, cols].bitcast(FP8X4),
                    scales=fs[:, g, cols],
                    in_=fg[half, g][:].rearrange("p q j -> p (q j)"),
                )

        def stage2(gi, t, j0, n, tag, bufs, groups=range(NG), acc=None):
            rows = slice(512 * gi + 128 * t, 512 * gi + 128 * t + 128)
            cols = slice(j0, j0 + n)
            if acc is None:
                acc = bank(tag, bufs)
            for g in groups:
                nc.tensor.matmul_mx(
                    out=acc[:, 0:n],
                    lhsT=fc[:, g, rows].bitcast(FP8X4),
                    lhsT_scale=fs[:, g, rows],
                    rhs=hc[:, g, cols].bitcast(FP8X4),
                    rhs_scale=hs[:, g, cols],
                    start=(g == 0),
                    stop=(g == NG - 1),
                )
            return acc

        def result(gi, t, j0, n, acc, engine="s"):
            dst = res[gi][:, t, j0 : j0 + n]
            if engine == "s":
                nc.scalar.activation(out=dst, in_=acc[:, 0:n], func=ACT.Copy, scale=-1.0 / ROOT_N)
            else:
                nc.vector.tensor_scalar(
                    out=dst, in0=acc[:, 0:n], scalar1=-1.0 / ROOT_N, scalar2=None, op0=MULT
                )
            if j0 // 512 == gi:
                q0, q1 = (j0 - 512 * gi) // 4, (j0 + n - 512 * gi) // 4
                diag = res[gi][:, t, j0 : j0 + n].rearrange("p (q s) -> p q s", s=4)[:, :, t]
                nc.gpsimd.tensor_tensor(out=diag, in0=diag, in1=root_i[:, q0:q1], op=ADD)

        rb = {}

        def out_cast(gi, j0, n, engine="v"):
            rb[gi, j0] = work.tile([P, 512, 4], BF16, name="rb", tag="rb", bufs=2, align_bytes=64)
            dst, src = rb[gi, j0][:, 0:n, :], res[gi][:, :, j0 : j0 + n].rearrange("p t j -> p j t")
            if engine == "v":
                nc.vector.tensor_copy(out=dst, in_=src)
            elif engine == "s":
                nc.scalar.copy(out=dst, in_=src)
            else:
                nc.gpsimd.tensor_scalar(out=dst, in0=src, scalar1=1.0, scalar2=0.0, op0=MULT, op1=ADD)
            dst = out_0[512 * gi : 512 * gi + 512, j0 : j0 + n].rearrange("(p t) j -> p t j", t=4)
            nc.sync.dma_start(out=dst, in_=res[gi][:, :, j0 : j0 + n])

        def out_quant(gi, j0, n):
            cols = slice(j0, j0 + n)
            nc.vector.quantize_mx(
                out=oc[gi][:, cols].bitcast(FP8X4),
                scales=out_s[:, gi, cols],
                in_=rb[gi, j0][:, 0:n, :].rearrange("p q j -> p (q j)"),
            )
            nc.sync.dma_start(
                out=out_1[gi, :, cols, :].rearrange("p m t -> p (m t)").bitcast(I32), in_=oc[gi][:, cols].bitcast(I32)
            )

        def out_scales():
            for q in range(4):
                nc.sync.dma_start(
                    out=out_2[:, 4 * q : 4 * q + 4, :].rearrange("g r n -> r g n").bitcast(I32),
                    in_=out_s[32 * q : 32 * q + 4, :, :].bitcast(I32),
                )

        for u, tag in ((0, "o"), (1, "tr")):
            for kp, engine in ((0, "s"), (1, "v")):
                x_transpose(0, kp, u, tag)
                x_copy(0, kp, u, engine)
            if u == 0:
                vectors_t()
            for kp in range(KP):
                x_quant(0, kp, 256 * u, 256)
        for piece in range(2):
            for l in range(2):
                stage1(0, l, piece)
            tanh(0, piece)
            if piece == 0:
                spread(0, "tr", "v")
        for u in range(2):
            x_transpose(1, 0, u)
            x_copy(1, 0, u, "s")

        x_plan = {0: (1, 1), 1: (2, 0), 2: (2, 1), 3: (3, 0), 4: (3, 1)}
        x_late = {1: (1, 1), 3: (2, 1), 5: (3, 1)}
        x_early = {0: (1, 0), 2: (2, 0), 4: (3, 0)}
        n_steps = len(steps)
        for s in range(n_steps + 1):
            more = s + 1 < n_steps
            if s in x_late:
                x_quant(*x_late[s])
            if more:
                stage1(s + 1, 0)
            if s in x_plan:
                x_transpose(*x_plan[s], 0)
            if s in x_plan:
                x_copy(*x_plan[s], 0, "s")
            if s in x_plan:
                x_transpose(*x_plan[s], 1)
            if s >= 1:
                transpose(fb, fp, s - 1)
            if more:
                stage1(s + 1, 1)
            if s in (3, 5):
                spread_late((s + 1) // 2)
            if s >= 1 and not late[s - 1]:
                transpose(hb, hp, s - 1)
            if s in x_plan:
                x_copy(*x_plan[s], 1, "s")
            if more:
                tanh(s + 1)
            if s == 0:
                spread(1, "tr", "s")
            if s < n_steps:
                elementwise(s)
            if s >= 2:
                f_quant(s - 2)
            if s >= 1:
                f_copy(s - 1)
            if s >= 2 and not late[s - 2]:
                h_quant(s - 2)
            if s >= 1 and not late[s - 1]:
                h_copy(s - 1)
            if s in x_early:
                x_quant(*x_early[s])
            if 10 <= s < 14:
                t = s - 10
                result(0, t, 0, 512, stage2(0, t, 0, 512, "o", 2), "s")
            if s in (14, 15):
                for t in (2 * (s - 14), 2 * (s - 14) + 1):
                    result(0, t, 512, 256, stage2(0, t, 512, 256, "o", 2), "s")

        slots = [0]

        def block_part(gi, t, j0, n, engine):
            tag, bufs = (("o", 2), ("y", 4), ("y", 4))[slots[0] % 3]
            slots[0] += 1
            result(gi, t, j0, n, stage2(gi, t, j0, n, tag, bufs), engine)

        def block(gi, j0, n, engines):
            for t in range(4):
                block_part(gi, t, j0, n, engines[t])

        def late_part(s):
            late_h(s)
            transpose(hb, hp, s)
            h_copy(s)

        late_h(12)
        acc0 = stage2(1, 0, 0, 512, "o", 2, range(2))
        acc1 = stage2(1, 1, 0, 512, "o", 2, range(2))
        acc2 = stage2(1, 2, 0, 512, "y", 4, range(2))
        late_h(13)
        transpose(hb, hp, 12)
        late_h(14)
        h_copy(12)
        transpose(hb, hp, 13)
        stage2(1, 0, 0, 512, "o", 2, range(2, 3), acc0)
        f_quant(15)
        late_h(15)
        acc3 = stage2(1, 3, 0, 512, "y", 4, range(2))
        stage2(1, 0, 0, 512, "o", 2, range(3, 4), acc0)
        transpose(hb, hp, 14)
        h_quant(12)
        out_cast(0, 0, 512, "v")
        h_copy(13)
        out_quant(0, 0, 512)
        out_cast(0, 512, 256, "v")
        transpose(hb, hp, 15)
        stage2(1, 2, 0, 512, "o", 2, range(2, 3), acc2)
        h_copy(14)
        stage2(1, 2, 0, 512, "o", 2, range(3, 4), acc2)
        stage2(1, 1, 0, 512, "o", 2, range(2, 3), acc1)
        result(1, 0, 0, 512, acc0, "s")
        stage2(1, 3, 0, 512, "o", 2, range(2, 3), acc3)
        h_copy(15)
        result(1, 2, 0, 512, acc2, "v")
        h_quant(14)
        stage2(1, 3, 0, 512, "o", 2, range(3, 4), acc3)
        stage2(1, 1, 0, 512, "o", 2, range(3, 4), acc1)
        result(1, 1, 0, 512, acc1, "s")
        result(1, 3, 0, 512, acc3, "s")
        h_quant(13)
        h_quant(15)
        block_part(1, 0, 512, 256, "s")
        out_quant(0, 512, 256)
        block_part(1, 1, 512, 256, "v")
        block_part(1, 2, 512, 256, "v")
        block_part(1, 3, 512, 256, "v")
        out_cast(1, 0, 512, "s")
        out_cast(1, 512, 256, "s")
        block_part(1, 0, 768, 256, "v")
        block_part(1, 1, 768, 256, "v")
        block_part(1, 2, 768, 256, "v")
        out_quant(1, 0, 512)
        block_part(1, 3, 768, 256, "s")
        block_part(0, 0, 768, 128, "s")
        out_quant(1, 512, 256)
        block_part(0, 1, 768, 128, "v")
        block_part(0, 2, 768, 128, "v")
        block_part(0, 3, 768, 128, "s")
        out_cast(0, 768, 128, "v")
        out_quant(0, 768, 128)
        block_part(0, 0, 896, 128, "v")
        block_part(0, 1, 896, 128, "s")
        out_cast(1, 768, 256, "v")
        block_part(0, 2, 896, 128, "s")
        out_quant(1, 768, 256)
        block_part(0, 3, 896, 128, "s")
        out_cast(0, 896, 128, "v")
        out_quant(0, 896, 128)
        out_scales()
